import numpy as np
import ml_dtypes


def mxq(x, axis, fmt="e4m3"):
    dtype, down = {"e4m3": (ml_dtypes.float8_e4m3fn, 7), "e5m2": (ml_dtypes.float8_e5m2, 14)}[fmt]
    v = np.moveaxis(np.asarray(x, np.float32).astype(ml_dtypes.bfloat16).astype(np.float64), axis, -1)
    blocks = v.reshape(v.shape[:-1] + (-1, 32))
    amax = np.abs(blocks).max(-1, keepdims=True)
    byte = np.maximum(np.where(amax > 0, np.frexp(amax)[1] - 1 + 127, 0) - down, 1)
    scale = np.exp2(byte - 127.0)
    codes = (blocks / scale).astype(np.float32).astype(dtype).astype(np.float64)
    return np.moveaxis((codes * scale).reshape(v.shape), -1, axis)


WIDE = False


def mx_kscale(k):
    if not WIDE:
        return np.ones(k)
    levels = np.array([10, -10, 5, -5, 0])
    if k % 512:
        return np.exp2(np.random.permutation(np.resize(levels, k // 32))).repeat(32)
    a = np.empty((k // 512, 16))
    for p in range(k // 512):
        a[p, :8] = np.random.permutation(np.resize(levels, 8))
        for g in range(8):
            far = levels[np.abs(levels - a[p, g]) >= 10]
            a[p, g + 8] = far[np.random.randint(len(far))]
    return np.exp2(a.ravel()).repeat(32)


def f64(x):
    return np.asarray(x).astype(np.float64)


def striped(idx):
    return np.tile(np.asarray(idx).reshape(-1, 16).T, (8, 1)).astype(np.uint16)


def unstriped(offs):
    return offs[:16].T.reshape(-1).astype(np.int64)


def striped8(idx):
    return np.asarray(idx).reshape(8, -1, 16).transpose(0, 2, 1).reshape(128, -1).astype(np.uint16)


def unstriped8(offs):
    return offs.reshape(8, 16, -1).transpose(0, 2, 1).reshape(8, -1).astype(np.int64)


def pick8(x, idx, run):
    r = np.arange(len(x))
    return x[r[:, None], idx[r % (8 * run) // run]]


E2M1 = np.array([0.0, 0.5, 1.0, 1.5, 2.0, 3.0, 4.0, 6.0, -0.0, -0.5, -1.0, -1.5, -2.0, -3.0, -4.0, -6.0])


def pack_weight(w, fmt):
    k, n = w.shape
    w = f64(np.asarray(w, np.float32).astype(ml_dtypes.bfloat16)).reshape(k // 32, 32, n)
    amax = np.abs(w).max(1)
    if fmt == "e4m3":
        byte = np.frexp(amax)[1] - 1 + 127 - 7
    else:
        mant, ex = np.frexp(amax / 6.0)
        byte = np.where(mant > 0.5, ex, ex - 1) + 127
    byte = np.clip(np.where(amax > 0, byte, 1), 1, 254)
    scaled = (w * np.exp2(127.0 - byte)[:, None, :]).reshape(k, n).astype(np.float32)
    by_word = np.ascontiguousarray(scaled.reshape(k // 512, 128, 4, n).transpose(0, 1, 3, 2))
    if fmt == "e4m3":
        words = by_word.astype(ml_dtypes.float8_e4m3fn).view(np.uint8)
    else:
        c = by_word.astype(ml_dtypes.float4_e2m1fn).view(np.uint8) & 0xF
        words = (c[..., 0::2] | (c[..., 1::2] << 4)).reshape(k // 512, 128, 2 * n)
    return np.ascontiguousarray(words), np.ascontiguousarray(byte.astype(np.uint8).reshape(k // 512, 16, n))


def unpack_weight(words, scales, fmt):
    g, _, n = scales.shape
    words = np.ascontiguousarray(words).reshape(g, 128, n, -1)
    if fmt == "e4m3":
        vals = words.view(ml_dtypes.float8_e4m3fn).astype(np.float64)
    else:
        nib = np.empty((g, 128, n, 4), np.uint8)
        nib[..., 0::2] = words & 0xF
        nib[..., 1::2] = words >> 4
        vals = E2M1[nib]
    vals = vals * np.repeat(np.exp2(scales.astype(np.float64) - 127.0), 8, axis=1)[..., None]
    return vals.transpose(0, 1, 3, 2).reshape(g * 512, n)


K, J, R, T, F, C, O, N, U, E = 512, 512, 512, 2048, 1024, 1024, 512, 256, 1024, 256


def setup_inputs():
    n = np.random.standard_normal
    idx = np.random.permutation(T)[:J]
    idx2 = np.random.permutation(F)[:R]
    idx3 = np.stack([np.random.permutation(C)[:J] for _ in range(8)])
    idx4 = np.stack([np.random.permutation(C)[:O] for _ in range(8)])
    idx5 = np.stack([np.random.permutation(U)[:O] for _ in range(8)])
    idx6 = np.stack([np.random.permutation(U)[:E] for _ in range(8)])
    idx7 = np.stack([np.random.permutation(U)[:E] for _ in range(8)])
    fk = mx_kscale(K)
    fr = mx_kscale(R)
    tr = np.ones(F)
    tr[idx2] = fr
    xtp = pack_weight(n((K, T)) * fk[:, None], "e2m1")
    wtp = pack_weight(n((K, F)) * 1 / np.sqrt(K) / fk[:, None] * tr, "e2m1")
    wbp = pack_weight(n((R, N)) * 1 / np.sqrt(R) / fr[:, None], "e4m3")
    return {
        "xt_words": xtp[0],
        "xt_scales": xtp[1],
        "wt_words": wtp[0],
        "wt_scales": wtp[1],
        "sa": (np.random.uniform(0.5, 1.6, (R, 1))).astype(np.float32),
        "wb_words": wbp[0],
        "wb_scales": wbp[1],
        "se": (np.random.uniform(0.5, 1.6, (N, 1))).astype(np.float32),
        "offs": striped(idx),
        "offs2": striped(idx2),
        "offs3": striped8(idx3),
        "offs4": striped8(idx4),
        "offs5": striped8(idx5),
        "offs6": striped8(idx6),
        "offs7": striped8(idx7),
    }


def reference(xt_words, xt_scales, wt_words, wt_scales, sa, wb_words, wb_scales, se, offs, offs2, offs3, offs4, offs5, offs6, offs7):
    idx = unstriped(offs)
    idx2 = unstriped(offs2)
    idx3 = unstriped8(offs3)
    idx4 = unstriped8(offs4)
    idx5 = unstriped8(offs5)
    idx6 = unstriped8(offs6)
    idx7 = unstriped8(offs7)
    xtu = unpack_weight(xt_words, xt_scales, "e2m1")
    wtu = unpack_weight(wt_words, wt_scales, "e2m1")
    wbu = unpack_weight(wb_words, wb_scales, "e4m3")
    wtidx2g = wtu[:, idx2]
    xtidxg = xtu[:, idx]
    a = wtidx2g.T @ xtidxg
    pw = np.zeros((R, C))
    pw[np.arange(R)[:, None], idx3[np.arange(R) % 512 // 64]] = a
    g1 = np.pad(pw, ((0, 0), (1, 0)))[:, :C]
    pg = np.abs(pw - g1)
    hid = pick8(pg, idx4, 64) * f64(sa)
    hidq = mxq(hid, 0, "e4m3")
    p = wbu.T @ hidq
    m0 = np.zeros((N, U))
    m0[np.arange(N)[:, None], idx5[np.arange(N) % 128 // 16]] = p
    m1 = pick8(m0, idx6, 16) * f64(se)
    m2 = np.zeros((N, U))
    m2[np.arange(N)[:, None], idx7[np.arange(N) % 128 // 16]] = m1
    y = m0 + m2
    return y

@@ -1,0 +1,238 @@
+from contextlib import ExitStack
+
+import concourse.mybir as mybir
+
+K, J, R, T, F, C, O, N, U, E = 512, 512, 512, 2048, 1024, 1024, 512, 256, 1024, 256
+FLOPS = 2 * K * R * J + 2 * R * N * O
+
+F32 = mybir.dt.float32
+BF16 = mybir.dt.bfloat16
+I32 = mybir.dt.int32
+U32 = mybir.dt.uint32
+U16 = mybir.dt.uint16
+U8 = mybir.dt.uint8
+FP4X4 = mybir.dt.float4_e2m1fn_x4
+FP8X4 = mybir.dt.float8_e4m3fn_x4
+ALU = mybir.AluOpType
+COPY = mybir.ActivationFunctionType.Copy
+
+P = 128
+PACK = 4
+STRIPE = 16
+ALIGN = 64
+HALF = 256
+O_PIECES = ((0, 128), (128, 256), (256, 512))
+LAST_STORE_PIECES = 4
+
+
+def tile_picked_tokens_store_one_steps_one_endecho_kernel(
+    tc, xt_words, xt_scales, wt_words, wt_scales, sa, wb_words, wb_scales, se,
+    offs, offs2, offs3, offs4, offs5, offs6, offs7, out,
+):
+    nc = tc.nc
+    with ExitStack() as ctx:
+        lists = ctx.enter_context(tc.tile_pool(name="lists", bufs=1))
+        sb = ctx.enter_context(tc.tile_pool(name="sb", bufs=1))
+        over = ctx.enter_context(tc.tile_pool(name="over", bufs=1))
+        ps = ctx.enter_context(tc.psum_pool(name="ps", bufs=1))
+
+        placed = {"diff00": 0, "diff01": 2560, "wd_w2": 1792, "wt_sc": 2240, "xg_w1": 2304, "xg_sc1": 2816, "wd_w1": 3072}
+
+        def new(name, shape, dtype, tag=None):
+            if name in placed:
+                return over.tile(shape, dtype, name=name, tag=name, align_bytes=ALIGN, offset=placed[name])
+            return sb.tile(shape, dtype, name=name, tag=tag or name, align_bytes=ALIGN)
+
+        def load_list(name, src):
+            tile = lists.tile(list(src.shape), U16, name=name, tag=name)
+            nc.sync.dma_start(tile[:], src)
+            return tile
+
+        def entries(tile, lo, hi):
+            return tile[:, lo // STRIPE : hi // STRIPE]
+
+        def load_scales(tile, src):
+            for q in range(4):
+                nc.sync.dma_start(tile[32 * q : 32 * q + 4, :].bitcast(I32), src[0, 4 * q : 4 * q + 4, :].bitcast(I32))
+
+        wt_sc = new("wt_sc", [P, F], U8)
+        xt_sc = new("xt_sc", [P, T], U8)
+        nc.gpsimd.memset(xt_sc[:].bitcast(I32), 0)
+        nc.gpsimd.memset(wt_sc[:].bitcast(I32), 0)
+        l2 = load_list("l2", offs2)
+        wt_w = new("wt_w", [P, 2 * F], U8)
+        nc.sync.dma_start(wt_w[:].bitcast(I32), wt_words[0].bitcast(I32))
+        l1 = load_list("l1", offs)
+        xt_w = new("xt_w", [P, 2 * T], U8)
+        nc.sync.dma_start(xt_w[:].bitcast(I32), xt_words[0].bitcast(I32))
+        load_scales(xt_sc, xt_scales)
+        load_scales(wt_sc, wt_scales)
+        l3 = load_list("l3", offs3)
+        board = [new(f"board{t}", [P, C], F32) for t in range(PACK)]
+        for t in range(PACK):
+            nc.gpsimd.memset(board[t][:], 0.0)
+        l4 = load_list("l4", offs4)
+        l5 = load_list("l5", offs5)
+        l6 = load_list("l6", offs6)
+        l7 = load_list("l7", offs7)
+
+        wg_w = new("wg_w", [P, 2 * R], U8)
+        wg_sc = new("wg_sc", [P, R], U8)
+        xg_w = [new(f"xg_w{h}", [P, 2 * HALF], U8) for h in range(2)]
+        xg_sc = [new(f"xg_sc{h}", [P, HALF], U8) for h in range(2)]
+
+        def gather_x_words(h):
+            nc.vector.tensor_copy(xg_w[h][:].bitcast(U16), xt_w[:].bitcast(U16).indirect(entries(l1, h * HALF, (h + 1) * HALF)))
+
+        def gather_x_scales(h):
+            nc.vector.tensor_copy(xg_sc[h][:], xt_sc[:].indirect(entries(l1, h * HALF, (h + 1) * HALF)))
+
+        wd_w, wd_sc = {}, {}
+
+        def deal_words(t0, t1):
+            tile = new(f"wd_w{t0}", [P, t1 - t0, 2 * P], U8)
+            nc.vector.tensor_copy(
+                tile[:].rearrange("p t (m b) -> p t m b", b=2),
+                wg_w[:].rearrange("p (m t b) -> p t m b", t=PACK, b=2)[:, t0:t1],
+            )
+            for t in range(t0, t1):
+                wd_w[t] = tile[:, t - t0, :]
+
+        def deal_scales(t0, t1):
+            tile = new(f"wd_sc{t0}", [P, t1 - t0, P], U8)
+            nc.vector.tensor_copy(tile[:], wg_sc[:].rearrange("p (m t) -> p t m", t=PACK)[:, t0:t1])
+            for t in range(t0, t1):
+                wd_sc[t] = tile[:, t - t0, :]
+
+        def first_product(acc, t, h):
+            nc.tensor.matmul_mx(
+                out=acc, lhsT=wd_w[t].bitcast(FP4X4), lhsT_scale=wd_sc[t],
+                rhs=xg_w[h][:].bitcast(FP4X4), rhs_scale=xg_sc[h][:], start=True, stop=True,
+            )
+
+        a_ps = {}
+        a_sb = {}
+
+        def product_half(t, h):
+            a_ps[t, h] = ps.tile([P, HALF], F32, name=f"a_ps{t}{h}", tag=f"bank{2 * t + h}")
+            first_product(a_ps[t, h][:], t, h)
+
+        def product_whole(t):
+            a_ps[t] = ps.tile([P, J], F32, name=f"a_ps{t}", tag=f"bank{t + 2}")
+            for h in range(2):
+                first_product(a_ps[t][:, h * HALF : (h + 1) * HALF], t, h)
+
+        def stage(key, width):
+            a_sb[key] = new("a_sb%d" % len(a_sb), [P, width], F32)
+            nc.vector.tensor_copy(a_sb[key][:], a_ps[key][:])
+
+        def put_on_board(t, key, lo, hi):
+            nc.scalar.activation(board[t][:].indirect(entries(l3, lo, hi)), a_sb[key][:], COPY)
+
+        nc.vector.tensor_copy(wg_w[:].bitcast(U16), wt_w[:].bitcast(U16).indirect(l2[:]))
+        gather_x_words(0)
+        gather_x_scales(0)
+        deal_words(0, 1)
+        nc.vector.tensor_copy(wg_sc[:], wt_sc[:].indirect(l2[:]))
+        deal_scales(0, 1)
+        product_half(0, 0)
+        a_sb[0, 0] = new("a_first", [P, HALF], F32)
+        nc.scalar.activation(a_sb[0, 0][:], a_ps[0, 0][:], COPY)
+        put_on_board(0, (0, 0), 0, HALF)
+        deal_words(1, 2)
+        deal_scales(1, 2)
+        product_half(1, 0)
+        gather_x_words(1)
+        stage((1, 0), HALF)
+        put_on_board(1, (1, 0), 0, HALF)
+        gather_x_scales(1)
+        deal_words(2, 4)
+        deal_scales(2, 4)
+        a_ps["late"] = ps.tile([P, 2 * HALF], F32, name="a_ps_late", tag="bank1")
+        for t in range(2):
+            first_product(a_ps["late"][:, t * HALF : (t + 1) * HALF], t, 1)
+        product_whole(2)
+        product_whole(3)
+        stage("late", 2 * HALF)
+        for t in range(2):
+            nc.scalar.activation(
+                board[t][:].indirect(entries(l3, HALF, J)), a_sb["late"][:, t * HALF : (t + 1) * HALF], COPY
+            )
+        for t in range(2, 4):
+            stage(t, J)
+            put_on_board(t, t, 0, J)
+
+        sa_sb = new("sa_sb", [P, PACK], F32, tag="a_first")
+        nc.sync.dma_start(sa_sb[:], sa.rearrange("(p t) o -> p (t o)", t=PACK))
+        wb_w = new("wb_w", [P, N], U32, tag="a_sb1")
+        nc.sync.dma_start(wb_w[:].bitcast(I32), wb_words[0].rearrange("p n t -> p (n t)").bitcast(I32))
+        wb_sc = new("wb_sc", [P, N], U8, tag="a_sb2")
+        nc.gpsimd.memset(wb_sc[:].bitcast(I32), 0)
+        load_scales(wb_sc, wb_scales)
+        se_sb = [new(f"se{n}", [P, 1], F32, tag=f"a_sb{3 + n}") for n in range(N // P)]
+        for n in range(N // P):
+            nc.sync.dma_start(se_sb[n][:], se[n * P : (n + 1) * P, :])
+
+        CH = 640
+        steps = []
+        hid_flat = [new(f"hid{h}", [P, PACK * HALF], BF16) for h in range(2)]
+        hid = [x[:].rearrange("p (t o) -> p t o", t=PACK) for x in hid_flat]
+        page = {}
+        for t in range(PACK):
+            pg = new(f"steps{t}", [P, C], F32)
+            left = new(f"diff{t}0", [P, CH], F32)
+            right = hid_flat[1][:, HALF:].bitcast(F32) if t == PACK - 1 else new(f"diff{t}1", [P, C - CH], F32)[:]
+            d = [left, right]
+            b = board[t]
+            nc.vector.tensor_copy(d[0][:, 0:1], b[:, 0:1])
+            nc.vector.tensor_tensor(d[0][:, 1:CH], b[:, 1:CH], b[:, 0 : CH - 1], ALU.subtract)
+            nc.vector.tensor_tensor(d[1], b[:, CH:C], b[:, CH - 1 : C - 1], ALU.subtract)
+            nc.vector.scalar_tensor_tensor(pg[:, 0:CH], d[0][:], -1.0, d[0][:], ALU.mult, ALU.max)
+            nc.vector.scalar_tensor_tensor(pg[:, CH:C], d[1], -1.0, d[1], ALU.mult, ALU.max)
+            steps.append(pg)
+            page[t] = new(f"page{t}", [P, U], F32, tag=f"board{t}")
+            nc.gpsimd.memset(page[t][:], 0.0)
+        m0 = [page[0], page[1]]
+        m2 = [page[2], page[3]]
+
+        for h in range(2):
+            for t in range(PACK):
+                nc.scalar.activation(
+                    hid[h][:, t, :], steps[t][:].indirect(entries(l4, h * HALF, (h + 1) * HALF)), COPY,
+                    scale=sa_sb[:, t : t + 1],
+                )
+
+        for i, (lo, hi) in enumerate(O_PIECES):
+            w = hi - lo
+            h, c0 = divmod(lo, HALF)
+            woven = new(f"woven{i}", [P, w, PACK], BF16, tag="codes1" if i == 2 else None)
+            nc.vector.tensor_copy(
+                woven[:].rearrange("p (c i) t -> p c t i", i=4),
+                hid[h][:, :, c0 : c0 + w].rearrange("p t (c i) -> p c t i", i=4),
+            )
+            codes = new(f"codes{i}", [P, w], U32)
+            scales = new(f"scales{i}", [P, w], U8)
+            nc.vector.quantize_mx(out=codes[:].bitcast(FP8X4), scales=scales[:], in_=woven[:].rearrange("p w t -> p (w t)"))
+            for n in range(N // P):
+                acc = ps.tile([P, w], F32, name=f"p_ps{i}{n}", tag=f"bank{2 * i + n}")
+                nc.tensor.matmul_mx(
+                    out=acc[:], lhsT=wb_w[:, n * P : (n + 1) * P].bitcast(FP8X4), lhsT_scale=wb_sc[:, n * P : (n + 1) * P],
+                    rhs=codes[:].bitcast(FP8X4), rhs_scale=scales[:], start=True, stop=True,
+                )
+                p_sb = new(f"p_sb{i}{n}", [P, w], F32)
+                nc.vector.tensor_copy(p_sb[:], acc[:])
+                nc.scalar.activation(m0[n][:].indirect(entries(l5, lo, hi)), p_sb[:], COPY)
+
+        m1 = [new(f"echo{n}", [P, E], F32) for n in range(N // P)]
+        for n in range(N // P):
+            nc.scalar.activation(m1[n][:], m0[n][:].indirect(l6[:]), COPY, scale=se_sb[n][:])
+        for n in range(N // P):
+            nc.scalar.activation(m2[n][:].indirect(l7[:]), m1[n][:], COPY)
+        for n in range(N // P):
+            pieces = LAST_STORE_PIECES if n == N // P - 1 else 1
+            w = U // pieces
+            for s in range(pieces):
+                cols = slice(s * w, (s + 1) * w)
+                y = new(f"y{n}{s}", [P, w], F32)
+                nc.vector.tensor_tensor(y[:], m0[n][:, cols], m2[n][:, cols], ALU.add)
+                nc.sync.dma_start(out[n * P : (n + 1) * P, cols], y[:])

@@ -70,7 +70,7 @@ def tile_picked_tokens_store_one_steps_one_endecho_kernel(
         l3 = load_list("l3", offs3)
         board = [new(f"board{t}", [P, C], F32) for t in range(PACK)]
         for t in range(PACK):
-            nc.gpsimd.memset(board[t][:], 0.0)
+            (nc.gpsimd if t < 2 else nc.vector).memset(board[t][:], 0.0)
         l4 = load_list("l4", offs4)
         l5 = load_list("l5", offs5)
         l6 = load_list("l6", offs6)
@@ -87,7 +87,7 @@ def tile_picked_tokens_store_one_steps_one_endecho_kernel(
         def gather_x_scales(h):
             nc.vector.tensor_copy(xg_sc[h][:], xt_sc[:].indirect(entries(l1, h * HALF, (h + 1) * HALF)))
 
-        wd_w, wd_sc = {}, {}
+        wd_w = {}
 
         def deal_words(t0, t1):
             tile = new(f"wd_w{t0}", [P, t1 - t0, 2 * P], U8)
@@ -98,15 +98,9 @@ def tile_picked_tokens_store_one_steps_one_endecho_kernel(
             for t in range(t0, t1):
                 wd_w[t] = tile[:, t - t0, :]
 
-        def deal_scales(t0, t1):
-            tile = new(f"wd_sc{t0}", [P, t1 - t0, P], U8)
-            nc.vector.tensor_copy(tile[:], wg_sc[:].rearrange("p (m t) -> p t m", t=PACK)[:, t0:t1])
-            for t in range(t0, t1):
-                wd_sc[t] = tile[:, t - t0, :]
-
         def first_product(acc, t, h):
             nc.tensor.matmul_mx(
-                out=acc, lhsT=wd_w[t].bitcast(FP4X4), lhsT_scale=wd_sc[t],
+                out=acc, lhsT=wd_w[t].bitcast(FP4X4), lhsT_scale=wg_sc[:, t * P : (t + 1) * P],
                 rhs=xg_w[h][:].bitcast(FP4X4), rhs_scale=xg_sc[h][:], start=True, stop=True,
             )
 
@@ -133,21 +127,18 @@ def tile_picked_tokens_store_one_steps_one_endecho_kernel(
         gather_x_words(0)
         gather_x_scales(0)
         deal_words(0, 1)
-        nc.vector.tensor_copy(wg_sc[:], wt_sc[:].indirect(l2[:]))
-        deal_scales(0, 1)
+        nc.vector.tensor_copy(wg_sc[:].rearrange("p (t m) -> p m t", t=PACK), wt_sc[:].indirect(l2[:]))
         product_half(0, 0)
         a_sb[0, 0] = new("a_first", [P, HALF], F32)
         nc.scalar.activation(a_sb[0, 0][:], a_ps[0, 0][:], COPY)
         put_on_board(0, (0, 0), 0, HALF)
         deal_words(1, 2)
-        deal_scales(1, 2)
         product_half(1, 0)
         gather_x_words(1)
         stage((1, 0), HALF)
         put_on_board(1, (1, 0), 0, HALF)
         gather_x_scales(1)
         deal_words(2, 4)
-        deal_scales(2, 4)
         a_ps["late"] = ps.tile([P, 2 * HALF], F32, name="a_ps_late", tag="bank1")
         for t in range(2):
             first_product(a_ps["late"][:, t * HALF : (t + 1) * HALF], t, 1)

@@ -36,7 +36,7 @@ def tile_picked_tokens_store_one_steps_one_endecho_kernel(
         over = ctx.enter_context(tc.tile_pool(name="over", bufs=1))
         ps = ctx.enter_context(tc.psum_pool(name="ps", bufs=1))
 
-        placed = {"diff00": 0, "diff01": 2560, "wd_w2": 1792, "wt_sc": 2240, "xg_w1": 2304, "xg_sc1": 2816, "wd_w1": 3072}
+        placed = {"page0": 0, "page1": 4096, "wd_w2": 3328, "wt_sc": 3776, "xg_w1": 3840, "xg_sc1": 4352, "wd_w1": 4608}
 
         def new(name, shape, dtype, tag=None):
             if name in placed:
@@ -168,7 +168,9 @@ def tile_picked_tokens_store_one_steps_one_endecho_kernel(
         steps = []
         hid_flat = [new(f"hid{h}", [P, PACK * HALF], BF16) for h in range(2)]
         hid = [x[:].rearrange("p (t o) -> p t o", t=PACK) for x in hid_flat]
-        page = {}
+        m0 = [new(f"page{n}", [P, U], F32) for n in range(N // P)]
+        for n in range(N // P):
+            nc.vector.memset(m0[n][:], 0.0)
         for t in range(PACK):
             pg = new(f"steps{t}", [P, C], F32)
             left = new(f"diff{t}0", [P, CH], F32)
@@ -181,10 +183,6 @@ def tile_picked_tokens_store_one_steps_one_endecho_kernel(
             nc.vector.scalar_tensor_tensor(pg[:, 0:CH], d[0][:], -1.0, d[0][:], ALU.mult, ALU.max)
             nc.vector.scalar_tensor_tensor(pg[:, CH:C], d[1], -1.0, d[1], ALU.mult, ALU.max)
             steps.append(pg)
-            page[t] = new(f"page{t}", [P, U], F32, tag=f"board{t}")
-            nc.gpsimd.memset(page[t][:], 0.0)
-        m0 = [page[0], page[1]]
-        m2 = [page[2], page[3]]
 
         for h in range(2):
             for t in range(PACK):
@@ -214,6 +212,9 @@ def tile_picked_tokens_store_one_steps_one_endecho_kernel(
                 nc.vector.tensor_copy(p_sb[:], acc[:])
                 nc.scalar.activation(m0[n][:].indirect(entries(l5, lo, hi)), p_sb[:], COPY)
 
+        m2 = [new(f"second{n}", [P, U], F32, tag=f"p_sb2{n}") for n in range(N // P)]
+        for n in range(N // P):
+            nc.vector.memset(m2[n][:], 0.0)
         m1 = [new(f"echo{n}", [P, E], F32) for n in range(N // P)]
         for n in range(N // P):
             nc.scalar.activation(m1[n][:], m0[n][:].indirect(l6[:]), COPY, scale=se_sb[n][:])

@@ -18,11 +18,23 @@ COPY = mybir.ActivationFunctionType.Copy
 
 P = 128
 PACK = 4
+QUADRANT = 32
 STRIPE = 16
 ALIGN = 64
 HALF = 256
-O_PIECES = ((0, 128), (128, 256), (256, 512))
-LAST_STORE_PIECES = 4
+OUT_TILES = N // P
+RUN = 4
+PLACE_PIECES = ((0, 128), (128, 256), (256, 512))
+LEFT = C - (PACK - 1) * HALF // 2
+LAST_STORE_EDGES = (0, 384, 704, 896, 1024)
+SHARED_BYTES = {
+    "page0": 0,
+    "page1": 4 * U,
+    "x_words1": 4 * U - HALF,
+    "x_scales1": 4 * U + HALF,
+    "w_dealt2": 4 * U - 3 * HALF,
+    "wt_scale_window": 4 * U - HALF - ALIGN,
+}
 
 
 def tile_picked_tokens_store_one_steps_one_endecho_kernel(
@@ -31,200 +43,205 @@ def tile_picked_tokens_store_one_steps_one_endecho_kernel(
 ):
     nc = tc.nc
     with ExitStack() as ctx:
-        lists = ctx.enter_context(tc.tile_pool(name="lists", bufs=1))
+        list_pool = ctx.enter_context(tc.tile_pool(name="lists", bufs=1))
         sb = ctx.enter_context(tc.tile_pool(name="sb", bufs=1))
-        over = ctx.enter_context(tc.tile_pool(name="over", bufs=1))
+        shared = ctx.enter_context(tc.tile_pool(name="shared", bufs=1))
         ps = ctx.enter_context(tc.psum_pool(name="ps", bufs=1))
 
-        placed = {"page0": 0, "page1": 4096, "wd_w2": 3328, "wt_sc": 3776, "xg_w1": 3840, "xg_sc1": 4352, "wd_w1": 4608}
+        def new(name, shape, dtype, after=None):
+            if name in SHARED_BYTES:
+                return shared.tile(shape, dtype, name=name, tag=name, align_bytes=ALIGN, offset=SHARED_BYTES[name])
+            return sb.tile(shape, dtype, name=name, tag=after or name, align_bytes=ALIGN)
 
-        def new(name, shape, dtype, tag=None):
-            if name in placed:
-                return over.tile(shape, dtype, name=name, tag=name, align_bytes=ALIGN, offset=placed[name])
-            return sb.tile(shape, dtype, name=name, tag=tag or name, align_bytes=ALIGN)
+        def bank(name, number, width):
+            return ps.tile([P, width], F32, name=name, tag=f"bank{number}")
 
-        def load_list(name, src):
-            tile = lists.tile(list(src.shape), U16, name=name, tag=name)
-            nc.sync.dma_start(tile[:], src)
-            return tile
+        def load_list(name, source):
+            offsets = list_pool.tile(list(source.shape), U16, name=name, tag=name)
+            nc.sync.dma_start(offsets[:], source)
+            return offsets
 
-        def entries(tile, lo, hi):
-            return tile[:, lo // STRIPE : hi // STRIPE]
+        def entries(offsets, first, end):
+            return offsets[:, first // STRIPE : end // STRIPE]
 
-        def load_scales(tile, src):
-            for q in range(4):
-                nc.sync.dma_start(tile[32 * q : 32 * q + 4, :].bitcast(I32), src[0, 4 * q : 4 * q + 4, :].bitcast(I32))
+        def load_scale_rows(target, source):
+            for q in range(P // QUADRANT):
+                nc.sync.dma_start(
+                    target[QUADRANT * q : QUADRANT * q + 4, :].bitcast(I32),
+                    source[0, 4 * q : 4 * q + 4, :].bitcast(I32),
+                )
 
-        wt_sc = new("wt_sc", [P, F], U8)
-        xt_sc = new("xt_sc", [P, T], U8)
-        nc.gpsimd.memset(xt_sc[:].bitcast(I32), 0)
-        nc.gpsimd.memset(wt_sc[:].bitcast(I32), 0)
-        l2 = load_list("l2", offs2)
-        wt_w = new("wt_w", [P, 2 * F], U8)
-        nc.sync.dma_start(wt_w[:].bitcast(I32), wt_words[0].bitcast(I32))
-        l1 = load_list("l1", offs)
-        xt_w = new("xt_w", [P, 2 * T], U8)
-        nc.sync.dma_start(xt_w[:].bitcast(I32), xt_words[0].bitcast(I32))
-        load_scales(xt_sc, xt_scales)
-        load_scales(wt_sc, wt_scales)
-        l3 = load_list("l3", offs3)
+        def half(h):
+            return slice(h * HALF, (h + 1) * HALF)
+
+        wt_scale_window = new("wt_scale_window", [P, F], U8)
+        xt_scale_window = new("xt_scale_window", [P, T], U8)
+        nc.gpsimd.memset(xt_scale_window[:].bitcast(I32), 0)
+        nc.gpsimd.memset(wt_scale_window[:].bitcast(I32), 0)
+        idx2 = load_list("idx2", offs2)
+        wt_word_window = new("wt_word_window", [P, 2 * F], U8)
+        nc.sync.dma_start(wt_word_window[:].bitcast(I32), wt_words[0].bitcast(I32))
+        idx = load_list("idx", offs)
+        load_scale_rows(xt_scale_window, xt_scales)
+        xt_word_window = new("xt_word_window", [P, 2 * T], U8)
+        nc.sync.dma_start(xt_word_window[:].bitcast(I32), xt_words[0].bitcast(I32))
+        load_scale_rows(wt_scale_window, wt_scales)
+        idx3 = load_list("idx3", offs3)
         board = [new(f"board{t}", [P, C], F32) for t in range(PACK)]
         for t in range(PACK):
-            (nc.gpsimd if t < 2 else nc.vector).memset(board[t][:], 0.0)
-        l4 = load_list("l4", offs4)
-        l5 = load_list("l5", offs5)
-        l6 = load_list("l6", offs6)
-        l7 = load_list("l7", offs7)
+            (nc.gpsimd if t < PACK // 2 else nc.vector).memset(board[t][:], 0.0)
+        idx4 = load_list("idx4", offs4)
+        idx5 = load_list("idx5", offs5)
+        idx6 = load_list("idx6", offs6)
+        idx7 = load_list("idx7", offs7)
 
-        wg_w = new("wg_w", [P, 2 * R], U8)
-        wg_sc = new("wg_sc", [P, R], U8)
-        xg_w = [new(f"xg_w{h}", [P, 2 * HALF], U8) for h in range(2)]
-        xg_sc = [new(f"xg_sc{h}", [P, HALF], U8) for h in range(2)]
+        w_words = new("w_words", [P, 2 * R], U8)
+        w_scales = new("w_scales", [P, R], U8)
+        x_words = [new(f"x_words{h}", [P, 2 * HALF], U8) for h in range(2)]
+        x_scales = [new(f"x_scales{h}", [P, HALF], U8) for h in range(2)]
+        w_dealt = {}
 
         def gather_x_words(h):
-            nc.vector.tensor_copy(xg_w[h][:].bitcast(U16), xt_w[:].bitcast(U16).indirect(entries(l1, h * HALF, (h + 1) * HALF)))
+            window = xt_word_window[:].bitcast(U16)
+            nc.vector.tensor_copy(x_words[h][:].bitcast(U16), window.indirect(entries(idx, h * HALF, (h + 1) * HALF)))
 
         def gather_x_scales(h):
-            nc.vector.tensor_copy(xg_sc[h][:], xt_sc[:].indirect(entries(l1, h * HALF, (h + 1) * HALF)))
+            nc.vector.tensor_copy(x_scales[h][:], xt_scale_window[:].indirect(entries(idx, h * HALF, (h + 1) * HALF)))
 
-        wd_w = {}
-
-        def deal_words(t0, t1):
-            tile = new(f"wd_w{t0}", [P, t1 - t0, 2 * P], U8)
+        def deal_w_words(first):
+            pair = new(f"w_dealt{first}", [P, 2, 2 * P], U8)
             nc.vector.tensor_copy(
-                tile[:].rearrange("p t (m b) -> p t m b", b=2),
-                wg_w[:].rearrange("p (m t b) -> p t m b", t=PACK, b=2)[:, t0:t1],
+                pair[:].rearrange("p t (m b) -> p t m b", b=2),
+                w_words[:].rearrange("p (m t b) -> p t m b", t=PACK, b=2)[:, first : first + 2],
             )
-            for t in range(t0, t1):
-                wd_w[t] = tile[:, t - t0, :]
+            w_dealt[first], w_dealt[first + 1] = pair[:, 0, :], pair[:, 1, :]
 
-        def first_product(acc, t, h):
+        def first_product(target, t, h):
             nc.tensor.matmul_mx(
-                out=acc, lhsT=wd_w[t].bitcast(FP4X4), lhsT_scale=wg_sc[:, t * P : (t + 1) * P],
-                rhs=xg_w[h][:].bitcast(FP4X4), rhs_scale=xg_sc[h][:], start=True, stop=True,
+                out=target,
+                lhsT=w_dealt[t].bitcast(FP4X4),
+                lhsT_scale=w_scales[:, t * P : (t + 1) * P],
+                rhs=x_words[h][:].bitcast(FP4X4),
+                rhs_scale=x_scales[h][:],
+                start=True,
+                stop=True,
             )
 
-        a_ps = {}
-        a_sb = {}
+        def put_on_board(t, values, first, end):
+            nc.scalar.activation(board[t][:].indirect(entries(idx3, first, end)), values, COPY)
 
-        def product_half(t, h):
-            a_ps[t, h] = ps.tile([P, HALF], F32, name=f"a_ps{t}{h}", tag=f"bank{2 * t + h}")
-            first_product(a_ps[t, h][:], t, h)
-
-        def product_whole(t):
-            a_ps[t] = ps.tile([P, J], F32, name=f"a_ps{t}", tag=f"bank{t + 2}")
-            for h in range(2):
-                first_product(a_ps[t][:, h * HALF : (h + 1) * HALF], t, h)
-
-        def stage(key, width):
-            a_sb[key] = new("a_sb%d" % len(a_sb), [P, width], F32)
-            nc.vector.tensor_copy(a_sb[key][:], a_ps[key][:])
-
-        def put_on_board(t, key, lo, hi):
-            nc.scalar.activation(board[t][:].indirect(entries(l3, lo, hi)), a_sb[key][:], COPY)
-
-        nc.vector.tensor_copy(wg_w[:].bitcast(U16), wt_w[:].bitcast(U16).indirect(l2[:]))
-        gather_x_words(0)
+        nc.vector.tensor_copy(w_words[:].bitcast(U16), wt_word_window[:].bitcast(U16).indirect(idx2[:]))
         gather_x_scales(0)
-        deal_words(0, 1)
-        nc.vector.tensor_copy(wg_sc[:].rearrange("p (t m) -> p m t", t=PACK), wt_sc[:].indirect(l2[:]))
-        product_half(0, 0)
-        a_sb[0, 0] = new("a_first", [P, HALF], F32)
-        nc.scalar.activation(a_sb[0, 0][:], a_ps[0, 0][:], COPY)
-        put_on_board(0, (0, 0), 0, HALF)
-        deal_words(1, 2)
-        product_half(1, 0)
+        gather_x_words(0)
+        deal_w_words(0)
+        nc.vector.tensor_copy(w_scales[:].rearrange("p (t m) -> p m t", t=PACK), wt_scale_window[:].indirect(idx2[:]))
+
+        a_early = []
+        for t in range(2):
+            acc = bank(f"a_early_acc{t}", t, HALF)
+            first_product(acc[:], t, 0)
+            a_early.append(new(f"a_early{t}", [P, HALF], F32))
+            nc.scalar.activation(a_early[t][:], acc[:], COPY)
+        for t in range(2):
+            put_on_board(t, a_early[t][:], 0, HALF)
         gather_x_words(1)
-        stage((1, 0), HALF)
-        put_on_board(1, (1, 0), 0, HALF)
         gather_x_scales(1)
-        deal_words(2, 4)
-        a_ps["late"] = ps.tile([P, 2 * HALF], F32, name="a_ps_late", tag="bank1")
+        deal_w_words(2)
+        a_late_acc = bank("a_late_acc", 2, 2 * HALF)
         for t in range(2):
-            first_product(a_ps["late"][:, t * HALF : (t + 1) * HALF], t, 1)
-        product_whole(2)
-        product_whole(3)
-        stage("late", 2 * HALF)
+            first_product(a_late_acc[:, half(t)], t, 1)
+        a_whole_acc = {t: bank(f"a_whole_acc{t}", t + 1, J) for t in range(2, PACK)}
+        for t in range(2, PACK):
+            for h in range(2):
+                first_product(a_whole_acc[t][:, half(h)], t, h)
+        a_late = new("a_late", [P, 2 * HALF], F32)
+        nc.vector.tensor_copy(a_late[:], a_late_acc[:])
         for t in range(2):
-            nc.scalar.activation(
-                board[t][:].indirect(entries(l3, HALF, J)), a_sb["late"][:, t * HALF : (t + 1) * HALF], COPY
-            )
-        for t in range(2, 4):
-            stage(t, J)
-            put_on_board(t, t, 0, J)
+            put_on_board(t, a_late[:, half(t)], HALF, J)
+        for t in range(2, PACK):
+            a_whole = new(f"a_whole{t}", [P, J], F32)
+            nc.vector.tensor_copy(a_whole[:], a_whole_acc[t][:])
+            put_on_board(t, a_whole[:], 0, J)
 
-        sa_sb = new("sa_sb", [P, PACK], F32, tag="a_first")
-        nc.sync.dma_start(sa_sb[:], sa.rearrange("(p t) o -> p (t o)", t=PACK))
-        wb_w = new("wb_w", [P, N], U32, tag="a_sb1")
-        nc.sync.dma_start(wb_w[:].bitcast(I32), wb_words[0].rearrange("p n t -> p (n t)").bitcast(I32))
-        wb_sc = new("wb_sc", [P, N], U8, tag="a_sb2")
-        nc.gpsimd.memset(wb_sc[:].bitcast(I32), 0)
-        load_scales(wb_sc, wb_scales)
-        se_sb = [new(f"se{n}", [P, 1], F32, tag=f"a_sb{3 + n}") for n in range(N // P)]
-        for n in range(N // P):
-            nc.sync.dma_start(se_sb[n][:], se[n * P : (n + 1) * P, :])
+        sa_rows = new("sa_rows", [P, PACK], F32, after="a_early0")
+        nc.sync.dma_start(sa_rows[:], sa.rearrange("(p t) o -> p (t o)", t=PACK))
+        wb_codes = new("wb_codes", [P, N], U32, after="a_early1")
+        nc.sync.dma_start(wb_codes[:].bitcast(I32), wb_words[0].rearrange("p n t -> p (n t)").bitcast(I32))
+        wb_scale_rows = new("wb_scale_rows", [P, N], U8, after="a_late")
+        nc.gpsimd.memset(wb_scale_rows[:].bitcast(I32), 0)
+        load_scale_rows(wb_scale_rows, wb_scales)
+        se_rows = [new(f"se_rows{b}", [P, 1], F32, after=f"a_whole{2 + b}") for b in range(OUT_TILES)]
+        for b in range(OUT_TILES):
+            nc.sync.dma_start(se_rows[b][:], se[b * P : (b + 1) * P, :])
 
-        CH = 640
-        steps = []
         hid_flat = [new(f"hid{h}", [P, PACK * HALF], BF16) for h in range(2)]
-        hid = [x[:].rearrange("p (t o) -> p t o", t=PACK) for x in hid_flat]
-        m0 = [new(f"page{n}", [P, U], F32) for n in range(N // P)]
-        for n in range(N // P):
-            nc.vector.memset(m0[n][:], 0.0)
+        hid = [flat[:].rearrange("p (t o) -> p t o", t=PACK) for flat in hid_flat]
+        page = [new(f"page{b}", [P, U], F32) for b in range(OUT_TILES)]
+        for b in range(OUT_TILES):
+            nc.vector.memset(page[b][:], 0.0)
+        steps = []
         for t in range(PACK):
-            pg = new(f"steps{t}", [P, C], F32)
-            left = new(f"diff{t}0", [P, CH], F32)
-            right = hid_flat[1][:, HALF:].bitcast(F32) if t == PACK - 1 else new(f"diff{t}1", [P, C - CH], F32)[:]
-            d = [left, right]
-            b = board[t]
-            nc.vector.tensor_copy(d[0][:, 0:1], b[:, 0:1])
-            nc.vector.tensor_tensor(d[0][:, 1:CH], b[:, 1:CH], b[:, 0 : CH - 1], ALU.subtract)
-            nc.vector.tensor_tensor(d[1], b[:, CH:C], b[:, CH - 1 : C - 1], ALU.subtract)
-            nc.vector.scalar_tensor_tensor(pg[:, 0:CH], d[0][:], -1.0, d[0][:], ALU.mult, ALU.max)
-            nc.vector.scalar_tensor_tensor(pg[:, CH:C], d[1], -1.0, d[1], ALU.mult, ALU.max)
-            steps.append(pg)
+            steps.append(new(f"steps{t}", [P, C], F32))
+            left = new(f"diff_left{t}", [P, LEFT], F32)[:]
+            if t == PACK - 1:
+                right = hid_flat[1][:, HALF:].bitcast(F32)
+            else:
+                right = new(f"diff_right{t}", [P, C - LEFT], F32)[:]
+            nc.vector.tensor_copy(left[:, 0:1], board[t][:, 0:1])
+            nc.vector.tensor_tensor(left[:, 1:LEFT], board[t][:, 1:LEFT], board[t][:, 0 : LEFT - 1], ALU.subtract)
+            nc.vector.tensor_tensor(right, board[t][:, LEFT:C], board[t][:, LEFT - 1 : C - 1], ALU.subtract)
+            nc.vector.scalar_tensor_tensor(steps[t][:, 0:LEFT], left, -1.0, left, ALU.mult, ALU.max)
+            nc.vector.scalar_tensor_tensor(steps[t][:, LEFT:C], right, -1.0, right, ALU.mult, ALU.max)
 
         for h in range(2):
             for t in range(PACK):
                 nc.scalar.activation(
-                    hid[h][:, t, :], steps[t][:].indirect(entries(l4, h * HALF, (h + 1) * HALF)), COPY,
-                    scale=sa_sb[:, t : t + 1],
+                    hid[h][:, t, :],
+                    steps[t][:].indirect(entries(idx4, h * HALF, (h + 1) * HALF)),
+                    COPY,
+                    scale=sa_rows[:, t : t + 1],
                 )
 
-        for i, (lo, hi) in enumerate(O_PIECES):
-            w = hi - lo
-            h, c0 = divmod(lo, HALF)
-            woven = new(f"woven{i}", [P, w, PACK], BF16, tag="codes1" if i == 2 else None)
+        last_piece = len(PLACE_PIECES) - 1
+        for i, (first, end) in enumerate(PLACE_PIECES):
+            width = end - first
+            h, start = divmod(first, HALF)
+            woven = new(f"woven{i}", [P, width, PACK], BF16, after=f"codes{i - 1}" if i == last_piece else None)
             nc.vector.tensor_copy(
-                woven[:].rearrange("p (c i) t -> p c t i", i=4),
-                hid[h][:, :, c0 : c0 + w].rearrange("p t (c i) -> p c t i", i=4),
+                woven[:].rearrange("p (c i) t -> p c t i", i=RUN),
+                hid[h][:, :, start : start + width].rearrange("p t (c i) -> p c t i", i=RUN),
             )
-            codes = new(f"codes{i}", [P, w], U32)
-            scales = new(f"scales{i}", [P, w], U8)
-            nc.vector.quantize_mx(out=codes[:].bitcast(FP8X4), scales=scales[:], in_=woven[:].rearrange("p w t -> p (w t)"))
-            for n in range(N // P):
-                acc = ps.tile([P, w], F32, name=f"p_ps{i}{n}", tag=f"bank{2 * i + n}")
+            codes = new(f"codes{i}", [P, width], U32)
+            scales = new(f"scales{i}", [P, width], U8)
+            nc.vector.quantize_mx(
+                out=codes[:].bitcast(FP8X4), scales=scales[:], in_=woven[:].rearrange("p o t -> p (o t)")
+            )
+            for b in range(OUT_TILES):
+                acc = bank(f"p_acc{i}{b}", OUT_TILES * i + b, width)
                 nc.tensor.matmul_mx(
-                    out=acc[:], lhsT=wb_w[:, n * P : (n + 1) * P].bitcast(FP8X4), lhsT_scale=wb_sc[:, n * P : (n + 1) * P],
-                    rhs=codes[:].bitcast(FP8X4), rhs_scale=scales[:], start=True, stop=True,
+                    out=acc[:],
+                    lhsT=wb_codes[:, b * P : (b + 1) * P].bitcast(FP8X4),
+                    lhsT_scale=wb_scale_rows[:, b * P : (b + 1) * P],
+                    rhs=codes[:].bitcast(FP8X4),
+                    rhs_scale=scales[:],
+                    start=True,
+                    stop=True,
                 )
-                p_sb = new(f"p_sb{i}{n}", [P, w], F32)
-                nc.vector.tensor_copy(p_sb[:], acc[:])
-                nc.scalar.activation(m0[n][:].indirect(entries(l5, lo, hi)), p_sb[:], COPY)
+                p_piece = new(f"p_piece{i}{b}", [P, width], F32)
+                nc.vector.tensor_copy(p_piece[:], acc[:])
+                nc.scalar.activation(page[b][:].indirect(entries(idx5, first, end)), p_piece[:], COPY)
 
-        m2 = [new(f"second{n}", [P, U], F32, tag=f"p_sb2{n}") for n in range(N // P)]
-        for n in range(N // P):
-            nc.vector.memset(m2[n][:], 0.0)
-        m1 = [new(f"echo{n}", [P, E], F32) for n in range(N // P)]
-        for n in range(N // P):
-            nc.scalar.activation(m1[n][:], m0[n][:].indirect(l6[:]), COPY, scale=se_sb[n][:])
-        for n in range(N // P):
-            nc.scalar.activation(m2[n][:].indirect(l7[:]), m1[n][:], COPY)
-        for n in range(N // P):
-            pieces = LAST_STORE_PIECES if n == N // P - 1 else 1
-            w = U // pieces
-            for s in range(pieces):
-                cols = slice(s * w, (s + 1) * w)
-                y = new(f"y{n}{s}", [P, w], F32)
-                nc.vector.tensor_tensor(y[:], m0[n][:, cols], m2[n][:, cols], ALU.add)
-                nc.sync.dma_start(out[n * P : (n + 1) * P, cols], y[:])
+        page2 = [new(f"page2_{b}", [P, U], F32, after=f"p_piece{last_piece}{b}") for b in range(OUT_TILES)]
+        for b in range(OUT_TILES):
+            nc.vector.memset(page2[b][:], 0.0)
+        echo = [new(f"echo{b}", [P, E], F32) for b in range(OUT_TILES)]
+        for b in range(OUT_TILES):
+            nc.scalar.activation(echo[b][:], page[b][:].indirect(idx6[:]), COPY, scale=se_rows[b][:])
+        for b in range(OUT_TILES):
+            nc.scalar.activation(page2[b][:].indirect(idx7[:]), echo[b][:], COPY)
+        for b in range(OUT_TILES):
+            edges = LAST_STORE_EDGES if b == OUT_TILES - 1 else (0, U)
+            for first, end in zip(edges[:-1], edges[1:]):
+                total = new(f"total{b}_{first}", [P, end - first], F32)
+                nc.vector.tensor_tensor(total[:], page[b][:, first:end], page2[b][:, first:end], ALU.add)
+                nc.sync.dma_start(out[b * P : (b + 1) * P, first:end], total[:])

from contextlib import ExitStack

import concourse.mybir as mybir

K, J, R, T, F, C, O, N, U, E = 512, 512, 512, 2048, 1024, 1024, 512, 256, 1024, 256
FLOPS = 2 * K * R * J + 2 * R * N * O

F32 = mybir.dt.float32
BF16 = mybir.dt.bfloat16
I32 = mybir.dt.int32
U32 = mybir.dt.uint32
U16 = mybir.dt.uint16
U8 = mybir.dt.uint8
FP4X4 = mybir.dt.float4_e2m1fn_x4
FP8X4 = mybir.dt.float8_e4m3fn_x4
ALU = mybir.AluOpType
COPY = mybir.ActivationFunctionType.Copy

P = 128
PACK = 4
QUADRANT = 32
STRIPE = 16
ALIGN = 64
HALF = 256
OUT_TILES = N // P
RUN = 4
PLACE_PIECES = ((0, 128), (128, 256), (256, 512))
LEFT = C - (PACK - 1) * HALF // 2
LAST_STORE_EDGES = (0, 384, 704, 896, 1024)
SHARED_BYTES = {
    "page0": 0,
    "page1": 4 * U,
    "x_words1": 4 * U - HALF,
    "x_scales1": 4 * U + HALF,
    "w_dealt2": 4 * U - 3 * HALF,
    "wt_scale_window": 4 * U - HALF - ALIGN,
}


def tile_picked_tokens_store_one_steps_one_endecho_kernel(
    tc, xt_words, xt_scales, wt_words, wt_scales, sa, wb_words, wb_scales, se,
    offs, offs2, offs3, offs4, offs5, offs6, offs7, out,
):
    nc = tc.nc
    with ExitStack() as ctx:
        list_pool = ctx.enter_context(tc.tile_pool(name="lists", bufs=1))
        sb = ctx.enter_context(tc.tile_pool(name="sb", bufs=1))
        shared = ctx.enter_context(tc.tile_pool(name="shared", bufs=1))
        ps = ctx.enter_context(tc.psum_pool(name="ps", bufs=1))

        def new(name, shape, dtype, after=None):
            if name in SHARED_BYTES:
                return shared.tile(shape, dtype, name=name, tag=name, align_bytes=ALIGN, offset=SHARED_BYTES[name])
            return sb.tile(shape, dtype, name=name, tag=after or name, align_bytes=ALIGN)

        def bank(name, number, width):
            return ps.tile([P, width], F32, name=name, tag=f"bank{number}")

        def load_list(name, source):
            offsets = list_pool.tile(list(source.shape), U16, name=name, tag=name)
            nc.sync.dma_start(offsets[:], source)
            return offsets

        def entries(offsets, first, end):
            return offsets[:, first // STRIPE : end // STRIPE]

        def load_scale_rows(target, source):
            for q in range(P // QUADRANT):
                nc.sync.dma_start(
                    target[QUADRANT * q : QUADRANT * q + 4, :].bitcast(I32),
                    source[0, 4 * q : 4 * q + 4, :].bitcast(I32),
                )

        def half(h):
            return slice(h * HALF, (h + 1) * HALF)

        wt_scale_window = new("wt_scale_window", [P, F], U8)
        xt_scale_window = new("xt_scale_window", [P, T], U8)
        nc.gpsimd.memset(xt_scale_window[:].bitcast(I32), 0)
        nc.gpsimd.memset(wt_scale_window[:].bitcast(I32), 0)
        idx2 = load_list("idx2", offs2)
        wt_word_window = new("wt_word_window", [P, 2 * F], U8)
        nc.sync.dma_start(wt_word_window[:].bitcast(I32), wt_words[0].bitcast(I32))
        idx = load_list("idx", offs)
        load_scale_rows(xt_scale_window, xt_scales)
        xt_word_window = new("xt_word_window", [P, 2 * T], U8)
        nc.sync.dma_start(xt_word_window[:].bitcast(I32), xt_words[0].bitcast(I32))
        load_scale_rows(wt_scale_window, wt_scales)
        idx3 = load_list("idx3", offs3)
        board = [new(f"board{t}", [P, C], F32) for t in range(PACK)]
        for t in range(PACK):
            (nc.gpsimd if t < PACK // 2 else nc.vector).memset(board[t][:], 0.0)
        idx4 = load_list("idx4", offs4)
        idx5 = load_list("idx5", offs5)
        idx6 = load_list("idx6", offs6)
        idx7 = load_list("idx7", offs7)

        w_words = new("w_words", [P, 2 * R], U8)
        w_scales = new("w_scales", [P, R], U8)
        x_words = [new(f"x_words{h}", [P, 2 * HALF], U8) for h in range(2)]
        x_scales = [new(f"x_scales{h}", [P, HALF], U8) for h in range(2)]
        w_dealt = {}

        def gather_x_words(h):
            window = xt_word_window[:].bitcast(U16)
            nc.vector.tensor_copy(x_words[h][:].bitcast(U16), window.indirect(entries(idx, h * HALF, (h + 1) * HALF)))

        def gather_x_scales(h):
            nc.vector.tensor_copy(x_scales[h][:], xt_scale_window[:].indirect(entries(idx, h * HALF, (h + 1) * HALF)))

        def deal_w_words(first):
            pair = new(f"w_dealt{first}", [P, 2, 2 * P], U8)
            nc.vector.tensor_copy(
                pair[:].rearrange("p t (m b) -> p t m b", b=2),
                w_words[:].rearrange("p (m t b) -> p t m b", t=PACK, b=2)[:, first : first + 2],
            )
            w_dealt[first], w_dealt[first + 1] = pair[:, 0, :], pair[:, 1, :]

        def first_product(target, t, h):
            nc.tensor.matmul_mx(
                out=target,
                lhsT=w_dealt[t].bitcast(FP4X4),
                lhsT_scale=w_scales[:, t * P : (t + 1) * P],
                rhs=x_words[h][:].bitcast(FP4X4),
                rhs_scale=x_scales[h][:],
                start=True,
                stop=True,
            )

        def put_on_board(t, values, first, end):
            nc.scalar.activation(board[t][:].indirect(entries(idx3, first, end)), values, COPY)

        nc.vector.tensor_copy(w_words[:].bitcast(U16), wt_word_window[:].bitcast(U16).indirect(idx2[:]))
        gather_x_scales(0)
        gather_x_words(0)
        deal_w_words(0)
        nc.vector.tensor_copy(w_scales[:].rearrange("p (t m) -> p m t", t=PACK), wt_scale_window[:].indirect(idx2[:]))

        a_early = []
        for t in range(2):
            acc = bank(f"a_early_acc{t}", t, HALF)
            first_product(acc[:], t, 0)
            a_early.append(new(f"a_early{t}", [P, HALF], F32))
            nc.scalar.activation(a_early[t][:], acc[:], COPY)
        for t in range(2):
            put_on_board(t, a_early[t][:], 0, HALF)
        gather_x_words(1)
        gather_x_scales(1)
        deal_w_words(2)
        a_late_acc = bank("a_late_acc", 2, 2 * HALF)
        for t in range(2):
            first_product(a_late_acc[:, half(t)], t, 1)
        a_whole_acc = {t: bank(f"a_whole_acc{t}", t + 1, J) for t in range(2, PACK)}
        for t in range(2, PACK):
            for h in range(2):
                first_product(a_whole_acc[t][:, half(h)], t, h)
        a_late = new("a_late", [P, 2 * HALF], F32)
        nc.vector.tensor_copy(a_late[:], a_late_acc[:])
        for t in range(2):
            put_on_board(t, a_late[:, half(t)], HALF, J)
        for t in range(2, PACK):
            a_whole = new(f"a_whole{t}", [P, J], F32)
            nc.vector.tensor_copy(a_whole[:], a_whole_acc[t][:])
            put_on_board(t, a_whole[:], 0, J)

        sa_rows = new("sa_rows", [P, PACK], F32, after="a_early0")
        nc.sync.dma_start(sa_rows[:], sa.rearrange("(p t) o -> p (t o)", t=PACK))
        wb_codes = new("wb_codes", [P, N], U32, after="a_early1")
        nc.sync.dma_start(wb_codes[:].bitcast(I32), wb_words[0].rearrange("p n t -> p (n t)").bitcast(I32))
        wb_scale_rows = new("wb_scale_rows", [P, N], U8, after="a_late")
        nc.gpsimd.memset(wb_scale_rows[:].bitcast(I32), 0)
        load_scale_rows(wb_scale_rows, wb_scales)
        se_rows = [new(f"se_rows{b}", [P, 1], F32, after=f"a_whole{2 + b}") for b in range(OUT_TILES)]
        for b in range(OUT_TILES):
            nc.sync.dma_start(se_rows[b][:], se[b * P : (b + 1) * P, :])

        hid_flat = [new(f"hid{h}", [P, PACK * HALF], BF16) for h in range(2)]
        hid = [flat[:].rearrange("p (t o) -> p t o", t=PACK) for flat in hid_flat]
        page = [new(f"page{b}", [P, U], F32) for b in range(OUT_TILES)]
        for b in range(OUT_TILES):
            nc.vector.memset(page[b][:], 0.0)
        steps = []
        for t in range(PACK):
            steps.append(new(f"steps{t}", [P, C], F32))
            left = new(f"diff_left{t}", [P, LEFT], F32)[:]
            if t == PACK - 1:
                right = hid_flat[1][:, HALF:].bitcast(F32)
            else:
                right = new(f"diff_right{t}", [P, C - LEFT], F32)[:]
            nc.vector.tensor_copy(left[:, 0:1], board[t][:, 0:1])
            nc.vector.tensor_tensor(left[:, 1:LEFT], board[t][:, 1:LEFT], board[t][:, 0 : LEFT - 1], ALU.subtract)
            nc.vector.tensor_tensor(right, board[t][:, LEFT:C], board[t][:, LEFT - 1 : C - 1], ALU.subtract)
            nc.vector.scalar_tensor_tensor(steps[t][:, 0:LEFT], left, -1.0, left, ALU.mult, ALU.max)
            nc.vector.scalar_tensor_tensor(steps[t][:, LEFT:C], right, -1.0, right, ALU.mult, ALU.max)

        for h in range(2):
            for t in range(PACK):
                nc.scalar.activation(
                    hid[h][:, t, :],
                    steps[t][:].indirect(entries(idx4, h * HALF, (h + 1) * HALF)),
                    COPY,
                    scale=sa_rows[:, t : t + 1],
                )

        last_piece = len(PLACE_PIECES) - 1
        for i, (first, end) in enumerate(PLACE_PIECES):
            width = end - first
            h, start = divmod(first, HALF)
            woven = new(f"woven{i}", [P, width, PACK], BF16, after=f"codes{i - 1}" if i == last_piece else None)
            nc.vector.tensor_copy(
                woven[:].rearrange("p (c i) t -> p c t i", i=RUN),
                hid[h][:, :, start : start + width].rearrange("p t (c i) -> p c t i", i=RUN),
            )
            codes = new(f"codes{i}", [P, width], U32)
            scales = new(f"scales{i}", [P, width], U8)
            nc.vector.quantize_mx(
                out=codes[:].bitcast(FP8X4), scales=scales[:], in_=woven[:].rearrange("p o t -> p (o t)")
            )
            for b in range(OUT_TILES):
                acc = bank(f"p_acc{i}{b}", OUT_TILES * i + b, width)
                nc.tensor.matmul_mx(
                    out=acc[:],
                    lhsT=wb_codes[:, b * P : (b + 1) * P].bitcast(FP8X4),
                    lhsT_scale=wb_scale_rows[:, b * P : (b + 1) * P],
                    rhs=codes[:].bitcast(FP8X4),
                    rhs_scale=scales[:],
                    start=True,
                    stop=True,
                )
                p_piece = new(f"p_piece{i}{b}", [P, width], F32)
                nc.vector.tensor_copy(p_piece[:], acc[:])
                nc.scalar.activation(page[b][:].indirect(entries(idx5, first, end)), p_piece[:], COPY)

        page2 = [new(f"page2_{b}", [P, U], F32, after=f"p_piece{last_piece}{b}") for b in range(OUT_TILES)]
        for b in range(OUT_TILES):
            nc.vector.memset(page2[b][:], 0.0)
        echo = [new(f"echo{b}", [P, E], F32) for b in range(OUT_TILES)]
        for b in range(OUT_TILES):
            nc.scalar.activation(echo[b][:], page[b][:].indirect(idx6[:]), COPY, scale=se_rows[b][:])
        for b in range(OUT_TILES):
            nc.scalar.activation(page2[b][:].indirect(idx7[:]), echo[b][:], COPY)
        for b in range(OUT_TILES):
            edges = LAST_STORE_EDGES if b == OUT_TILES - 1 else (0, U)
            for first, end in zip(edges[:-1], edges[1:]):
                total = new(f"total{b}_{first}", [P, end - first], F32)
                nc.vector.tensor_tensor(total[:], page[b][:, first:end], page2[b][:, first:end], ALU.add)
                nc.sync.dma_start(out[b * P : (b + 1) * P, first:end], total[:])
